import numpy as np
import ml_dtypes


def mxq(x, axis, fmt="e4m3"):
    dtype, down = {"e4m3": (ml_dtypes.float8_e4m3fn, 7), "e5m2": (ml_dtypes.float8_e5m2, 14)}[fmt]
    v = np.moveaxis(np.asarray(x, np.float32).astype(ml_dtypes.bfloat16).astype(np.float64), axis, -1)
    blocks = v.reshape(v.shape[:-1] + (-1, 32))
    amax = np.abs(blocks).max(-1, keepdims=True)
    byte = np.maximum(np.where(amax > 0, np.frexp(amax)[1] - 1 + 127, 0) - down, 1)
    scale = np.exp2(byte - 127.0)
    codes = (blocks / scale).astype(np.float32).astype(dtype).astype(np.float64)
    return np.moveaxis((codes * scale).reshape(v.shape), -1, axis)


WIDE = False


def mx_kscale(k):
    if not WIDE:
        return np.ones(k)
    levels = np.array([10, -10, 5, -5, 0])
    if k % 512:
        return np.exp2(np.random.permutation(np.resize(levels, k // 32))).repeat(32)
    a = np.empty((k // 512, 16))
    for p in range(k // 512):
        a[p, :8] = np.random.permutation(np.resize(levels, 8))
        for g in range(8):
            far = levels[np.abs(levels - a[p, g]) >= 10]
            a[p, g + 8] = far[np.random.randint(len(far))]
    return np.exp2(a.ravel()).repeat(32)


def f64(x):
    return np.asarray(x).astype(np.float64)


def striped(idx):
    return np.tile(idx.reshape(-1, 16).T, (8, 1)).astype(np.uint16)


def unstriped(offs):
    return offs[:16].T.reshape(-1).astype(np.int64)


def striped8(idx):
    return np.concatenate([x.reshape(-1, 16).T for x in idx]).astype(np.uint16)


def runs(offs, k):
    lists = np.stack([offs[16 * r : 16 * r + 16].T.reshape(-1) for r in range(8)]).astype(np.int64)
    return lists[np.arange(k) % 512 // 64]


def pack_weight(w):
    k, n = w.shape
    w = f64(np.asarray(w, np.float32).astype(ml_dtypes.bfloat16)).reshape(k // 32, 32, n)
    amax = np.abs(w).max(1)
    byte = np.clip(np.where(amax > 0, np.frexp(amax)[1] - 1 + 127 - 7, 1), 1, 254)
    scaled = (w * np.exp2(127.0 - byte)[:, None, :]).reshape(k, n).astype(np.float32)
    words = np.ascontiguousarray(scaled.reshape(k // 512, 128, 4, n).transpose(0, 1, 3, 2)).astype(ml_dtypes.float8_e4m3fn).view(np.uint8)
    return words, np.ascontiguousarray(byte.astype(np.uint8).reshape(k // 512, 16, n))


def unpack_weight(words, scales):
    g, p, n, _ = words.shape
    vals = np.ascontiguousarray(words).view(ml_dtypes.float8_e4m3fn).astype(np.float64) * np.repeat(np.exp2(scales.astype(np.float64) - 127.0), 8, axis=1)[..., None]
    return vals.transpose(0, 1, 3, 2).reshape(g * 512, n)


def sigmoid(v):
    return 1.0 / (1.0 + np.exp(-np.maximum(v, -700.0)))

def planes(y):
    n, m = y.shape
    v = y.astype(np.float32).astype(ml_dtypes.bfloat16).astype(np.float64).reshape(n // 32, 32, m)
    top = np.abs(v).max(1)
    byte = np.clip(np.where(top > 0, np.frexp(top)[1] - 1 + 127 - 7, 1), 1, 254)
    codes = (v * np.exp2(127.0 - byte)[:, None, :]).reshape(n, m).astype(np.float32).astype(ml_dtypes.float8_e4m3fn).view(np.uint8)
    words = codes.reshape(n // 512, 128, 4, m).transpose(0, 1, 3, 2)
    return np.ascontiguousarray(words), np.ascontiguousarray(byte.astype(np.uint8).reshape(n // 512, 16, m))


K, T, S, N, H, G = 512, 2048, 512, 512, 512, 2048


def setup_inputs():
    n = np.random.standard_normal
    s = mx_kscale(K)[:, None]
    u = mx_kscale(S)
    packed_xT = pack_weight(n((K, T)) * s)
    packed_w1 = pack_weight(n((K, H)) / np.sqrt(K) / s)
    packed_dT = pack_weight(n((K, G)) / s)
    packed_w2 = pack_weight(n((H, N)) / np.sqrt(H) / u[:, None])
    return {
        "x_words": packed_xT[0],
        "x_scales": packed_xT[1],
        "w1_words": packed_w1[0],
        "w1_scales": packed_w1[1],
        "d_words": packed_dT[0],
        "d_scales": packed_dT[1],
        "gn": (np.random.uniform(0.5, 1.5, (H, 1)) * u[:, None]).astype(np.float32),
        "w2_words": packed_w2[0],
        "w2_scales": packed_w2[1],
        "offs": striped(np.random.permutation(T)[:S]),
        "k1": striped8(np.random.randint(0, G, (8, H))),
        "two": striped(np.random.permutation(T)[:S]),
        "n1": striped(np.random.permutation(S)),
        "n2": striped(np.random.permutation(S)),
        "n3": striped(np.random.permutation(S)),
        "n4": striped(np.random.permutation(S)),
    }


def reference(x_words, x_scales, w1_words, w1_scales, d_words, d_scales, gn, w2_words, w2_scales, offs, k1, two, n1, n2, n3, n4):
    xq = unpack_weight(x_words, x_scales)[:, unstriped(offs)]
    y = unpack_weight(w1_words, w1_scales).T @ xq
    d_k1 = unpack_weight(d_words, d_scales)[np.arange(K)[:, None], runs(k1, K)]
    x_two = unpack_weight(x_words, x_scales)[:, unstriped(two)]
    d = 0.0625 * (d_k1.T @ x_two)
    z = f64(gn) * (y * (np.tanh(d[:, unstriped(n1)] - d[:, unstriped(n2)])))
    h = unpack_weight(w2_words, w2_scales).T @ mxq(z, 0, "e4m3")
    out_0 = h + (sigmoid(h[:, unstriped(n3)])) * (h[:, unstriped(n4)] - h)
    return (out_0,) + planes(out_0)

@@ -1,0 +1,212 @@
+from contextlib import ExitStack
+
+import concourse.mybir as mybir
+
+K, T, S, N, H, G = 512, 2048, 512, 512, 512, 2048
+FLOPS = 2 * K * H * S * 2 + 2 * H * N * S
+
+F32 = mybir.dt.float32
+BF16 = mybir.dt.bfloat16
+I32 = mybir.dt.int32
+U32 = mybir.dt.uint32
+U16 = mybir.dt.uint16
+U8 = mybir.dt.uint8
+FP8X4 = mybir.dt.float8_e4m3fn_x4
+ACT = mybir.ActivationFunctionType
+ALU = mybir.AluOpType
+
+P = 128
+PACK = 4
+A_CHUNKS = [256, 128, 128]
+A_SKEW = 3
+B_CHUNKS = [128, 256, 128]
+
+
+def chunk_slices(widths):
+    starts = [sum(widths[:c]) for c in range(len(widths))]
+    return [slice(a, a + w) for a, w in zip(starts, widths)]
+
+
+def entries(list_tile, cols):
+    return list_tile[:, cols.start // 16 : cols.stop // 16]
+
+
+def words_of(dram):
+    return dram[0].rearrange("p n t -> p (n t)").bitcast(I32)
+
+
+def deal(engine_copy, dst, src, run):
+    engine_copy(
+        out=dst[:].rearrange("p (t c i) -> p c t i", t=PACK, i=run),
+        in_=src[:].rearrange("p (c i t) -> p c t i", t=PACK, i=run),
+    )
+
+
+def interleave(engine_copy, dst, src):
+    engine_copy(out=dst[:].rearrange("p (c i) t -> p c t i", i=4), in_=src[:].rearrange("p t (c i) -> p c t i", i=4))
+
+
+def tile_picked_twkeyjointbtrack_none_po_kernel(
+    tc, x_words, x_scales, w1_words, w1_scales, d_words, d_scales, gn, w2_words, w2_scales, offs, k1, two, n1, n2, n3, n4, out_0, out_1, out_2
+):
+    nc = tc.nc
+    with ExitStack() as ctx:
+        lists = ctx.enter_context(tc.tile_pool(name="lists", bufs=1))
+        keep = ctx.enter_context(tc.tile_pool(name="keep", bufs=1))
+        psum = ctx.enter_context(tc.psum_pool(name="psum", bufs=1))
+
+        def load_list(name, dram):
+            held = lists.tile([P, S // 16], U16, name=name)
+            nc.sync.dma_start(held[:], dram)
+            return held
+
+        k1_l = load_list("k1_l", k1)
+        ds_win = keep.tile([P, G], U8, name="ds_win", align_bytes=64)
+        ds_src = d_scales[0].bitcast(I32).rearrange("(g e) c -> e g c", e=2)
+        for e in range(2):
+            nc.sync.dma_start(out=ds_win[e:P:2, :].bitcast(I32), in_=ds_src[e].unsqueeze(1).to_broadcast([8, 8, G // 4]))
+        xs_win = keep.tile([P, T], U8, name="xs_win", align_bytes=64)
+        xs_src = x_scales[0].bitcast(I32).rearrange("(q r) c -> r q c", r=4)
+        for r in range(4):
+            queue = nc.gpsimd if r == 3 else nc.sync
+            queue.dma_start(out=xs_win[r:P:4, :].bitcast(I32), in_=xs_src[r].unsqueeze(1).to_broadcast([4, 8, T // 4]))
+        two_l = load_list("two_l", two)
+        dw_win = keep.tile([P, G], U32, name="dw_win", align_bytes=64)
+        nc.sync.dma_start(out=dw_win[:].bitcast(I32), in_=words_of(d_words))
+        offs_l = load_list("offs_l", offs)
+        n2_l = load_list("n2_l", n2)
+        ws_raw = keep.tile([P, H], U8, name="ws_raw", tag="slot_b", align_bytes=64)
+
+        def load_weight_scales(rows):
+            for row in rows:
+                src = (w1_scales, w2_scales)[row // 4][0].bitcast(I32).rearrange("(q r) c -> r q c", r=4)
+                nc.sync.dma_start(out=ws_raw[row:P:8, :].bitcast(I32), in_=src[row % 4].unsqueeze(1).to_broadcast([4, 4, H // 4]))
+
+        load_weight_scales(range(2))
+        w1_raw = keep.tile([P, H], U32, name="w1_raw", tag="slot_a", align_bytes=64)
+        nc.sync.dma_start(out=w1_raw[:].bitcast(I32), in_=words_of(w1_words))
+        xw_win = keep.tile([P, T], U32, name="xw_win", align_bytes=64)
+        nc.sync.dma_start(out=xw_win[:].bitcast(I32), in_=words_of(x_words))
+        gain = keep.tile([P, PACK], F32, name="gain")
+        nc.gpsimd.dma_start(out=gain[:], in_=gn.rearrange("(p t) o -> p (t o)", t=PACK))
+
+        ds_placed = keep.tile([P, H], U8, name="ds_placed", align_bytes=64)
+        nc.vector.memset(ds_placed[:].bitcast(I32), 0)
+        ds_got = keep.tile([P, H], U8, name="ds_got", align_bytes=64)
+        nc.vector.tensor_copy(out=ds_got[:], in_=ds_win[:].indirect(k1_l[:]))
+        ds_dealt = keep.tile([P, H], U8, name="ds_dealt", align_bytes=64)
+        deal(nc.vector.tensor_copy, ds_dealt, ds_got, 16)
+        nc.scalar.dma_start(out=ds_placed[0:112, :].bitcast(I32), in_=ds_dealt[14:126, :].bitcast(I32))
+
+        xs_two = keep.tile([P, S], U8, name="xs_two", align_bytes=64)
+        nc.vector.tensor_copy(out=xs_two[:], in_=xs_win[:].indirect(two_l[:]))
+        dw_got = keep.tile([P, H], U32, name="dw_got", align_bytes=64)
+        nc.vector.tensor_copy(out=dw_got[:], in_=dw_win[:].indirect(k1_l[:]))
+        dw_dealt = keep.tile([P, H], U32, name="dw_dealt", align_bytes=64)
+        deal(nc.vector.tensor_copy, dw_dealt, dw_got, 4)
+        xw_two = keep.tile([P, S], U32, name="xw_two", align_bytes=64)
+        nc.vector.tensor_copy(out=xw_two[:], in_=xw_win[:].indirect(two_l[:]))
+
+        d_ps = [psum.tile([P, S], F32, name=f"d_ps{t}", tag=f"bank{t}") for t in range(PACK)]
+        for t in range(PACK):
+            m = slice(t * P, (t + 1) * P)
+            nc.tensor.matmul_mx(out=d_ps[t][:], lhsT=dw_dealt[:, m].bitcast(FP8X4), lhsT_scale=ds_placed[:, m],
+                                rhs=xw_two[:].bitcast(FP8X4), rhs_scale=xs_two[:], start=True, stop=True)
+
+        xs_idx = keep.tile([P, S], U8, name="xs_idx", align_bytes=64)
+        nc.vector.tensor_copy(out=xs_idx[:], in_=xs_win[:].indirect(offs_l[:]))
+        xw_idx = keep.tile([P, S], U32, name="xw_idx", align_bytes=64)
+        nc.vector.tensor_copy(out=xw_idx[:], in_=xw_win[:].indirect(offs_l[:]))
+
+        load_weight_scales(range(2, 8))
+        n1_l = load_list("n1_l", n1)
+        w2_raw = keep.tile([P, N], U32, name="w2_raw", tag="slot_c", align_bytes=64)
+        nc.sync.dma_start(out=w2_raw[:].bitcast(I32), in_=words_of(w2_words))
+        n3_l = load_list("n3_l", n3)
+        n4_l = load_list("n4_l", n4)
+        w1_dealt = keep.tile([P, H], U32, name="w1_dealt", align_bytes=64)
+        deal(nc.scalar.copy, w1_dealt, w1_raw, 4)
+        ws_dealt = keep.tile([P, H], U8, name="ws_dealt", align_bytes=64)
+        deal(nc.vector.tensor_copy, ws_dealt, ws_raw, 16)
+
+        y_ps = [psum.tile([P, S], F32, name=f"y_ps{t}", tag=f"bank{PACK + t}") for t in range(PACK)]
+        for t in range(PACK):
+            m = slice(t * P, (t + 1) * P)
+            nc.tensor.matmul_mx(out=y_ps[t][:], lhsT=w1_dealt[:, m].bitcast(FP8X4), lhsT_scale=ws_dealt[:, m],
+                                rhs=xw_idx[:].bitcast(FP8X4), rhs_scale=xs_idx[:], start=True, stop=True)
+
+        d_win = [keep.tile([P, S], F32, name=f"d_win{t}", tag="slot_a" if t == 0 else f"d_win{t}", align_bytes=64) for t in range(PACK)]
+        h_win = [keep.tile([P, S], F32, name=f"h_win{t}") for t in range(PACK)]
+        h_ps = [psum.tile([P, S], F32, name=f"h_ps{t}", tag=f"bank{t}") for t in range(PACK)]
+        w2_dealt = keep.tile([P, N], U32, name="w2_dealt", align_bytes=64)
+
+        for c, cols in enumerate(chunk_slices(A_CHUNKS)):
+            width = cols.stop - cols.start
+            d_two = keep.tile([P, PACK, width], F32, name=f"d_two{c}", tag="slot_c" if c == 1 else f"d_two{c}", align_bytes=64)
+            diff = keep.tile([P, PACK, width], F32, name=f"diff{c}", tag="slot_b" if c == 0 else f"diff{c}", align_bytes=64)
+            bend = keep.tile([P, PACK, width], F32, name=f"bend{c}")
+            z_rows = keep.tile([P, PACK, width], BF16, name=f"z_rows{c}")
+            for t in range(PACK + A_SKEW):
+                if t < PACK:
+                    if c == 0:
+                        nc.scalar.copy(out=d_win[t][:], in_=d_ps[t][:])
+                    nc.scalar.activation(out=d_two[:, t, :], in_=d_win[t][:].indirect(entries(n2_l, cols)), func=ACT.Copy)
+                    nc.vector.tensor_tensor(out=diff[:, t, :], in0=d_win[t][:].indirect(entries(n1_l, cols)), in1=d_two[:, t, :], op=ALU.subtract)
+                if t >= A_SKEW:
+                    u = t - A_SKEW
+                    nc.scalar.activation(out=bend[:, u, :], in_=diff[:, u, :], func=ACT.Tanh, scale=0.0625)
+                    nc.vector.scalar_tensor_tensor(out=z_rows[:, u, :], in0=y_ps[u][:, cols], scalar=gain[:, u : u + 1], in1=bend[:, u, :], op0=ALU.mult, op1=ALU.mult)
+            if c == 0:
+                deal(nc.scalar.copy, w2_dealt, w2_raw, 4)
+            z_packed = keep.tile([P, width, PACK], BF16, name=f"z_packed{c}", align_bytes=64)
+            interleave(nc.scalar.copy if c == 1 else nc.vector.tensor_copy, z_packed, z_rows)
+            z_words = keep.tile([P, width], U32, name=f"z_words{c}", align_bytes=64)
+            z_scales = keep.tile([P, width], U8, name=f"z_scales{c}", align_bytes=64)
+            nc.vector.quantize_mx(out=z_words[:].bitcast(FP8X4), scales=z_scales[:], in_=z_packed[:].rearrange("p n t -> p (n t)"))
+            for t in range(PACK):
+                m = slice(t * P, (t + 1) * P)
+                nc.tensor.matmul_mx(out=h_ps[t][:, cols], lhsT=w2_dealt[:, m].bitcast(FP8X4), lhsT_scale=ws_dealt[4:P, m],
+                                    rhs=z_words[:].bitcast(FP8X4), rhs_scale=z_scales[:], start=True, stop=True)
+            for t in range(PACK):
+                leave = nc.vector.tensor_copy if (c == len(A_CHUNKS) - 1 and t > 0) else nc.scalar.copy
+                leave(out=h_win[t][:, cols], in_=h_ps[t][:, cols])
+
+        out_rows = out_0.rearrange("(p t) n -> p t n", t=PACK)
+        o_words = keep.tile([P, S], U32, name="o_words", align_bytes=64)
+        o_scales = keep.tile([P, S], U8, name="o_scales", align_bytes=64)
+        words_out = words_of(out_1)
+        for c, cols in enumerate(chunk_slices(B_CHUNKS)):
+            width = cols.stop - cols.start
+            gate = keep.tile([P, PACK, width], F32, name=f"gate{c}")
+            got = keep.tile([P, PACK, width], F32, name=f"got{c}") if c == 1 else None
+            far = keep.tile([P, PACK, width], F32, name=f"far{c}")
+            near = keep.tile([P, PACK, width], F32, name=f"near{c}")
+            mixed = keep.tile([P, PACK, width], F32, name=f"mixed{c}")
+            for t in range(PACK + 1):
+                if t < PACK:
+                    nc.scalar.activation(out=gate[:, t, :], in_=h_win[t][:].indirect(entries(n3_l, cols)), func=ACT.Sigmoid)
+                    if c == 1:
+                        nc.scalar.activation(out=got[:, t, :], in_=h_win[t][:].indirect(entries(n4_l, cols)), func=ACT.Copy)
+                        nc.vector.tensor_tensor(out=near[:, t, :], in0=got[:, t, :], in1=h_win[t][:, cols], op=ALU.subtract)
+                        nc.vector.tensor_tensor(out=far[:, t, :], in0=near[:, t, :], in1=gate[:, t, :], op=ALU.mult)
+                    else:
+                        nc.vector.tensor_tensor(out=far[:, t, :], in0=h_win[t][:].indirect(entries(n4_l, cols)), in1=gate[:, t, :], op=ALU.mult)
+                        nc.vector.scalar_tensor_tensor(out=near[:, t, :], in0=gate[:, t, :], scalar=1.0, in1=h_win[t][:, cols], op0=ALU.subtract, op1=ALU.mult)
+                if t > 0:
+                    u = t - 1
+                    if c == 1:
+                        nc.vector.tensor_tensor(out=mixed[:, u, :], in0=far[:, u, :], in1=h_win[u][:, cols], op=ALU.add)
+                        if u % 2 == 1:
+                            nc.sync.dma_start(out=out_rows[:, u - 1 : u + 1, cols], in_=mixed[:, u - 1 : u + 1, :])
+                    else:
+                        nc.vector.tensor_tensor(out=mixed[:, u, :], in0=far[:, u, :], in1=near[:, u, :], op=ALU.subtract)
+            if c != 1:
+                nc.sync.dma_start(out=out_rows[:, :, cols], in_=mixed[:])
+            o_packed = keep.tile([P, width, PACK], BF16, name=f"o_packed{c}", align_bytes=64)
+            interleave(nc.scalar.copy if c == 1 else nc.vector.tensor_copy, o_packed, mixed)
+            nc.vector.quantize_mx(out=o_words[:, cols].bitcast(FP8X4), scales=o_scales[:, cols], in_=o_packed[:].rearrange("p n t -> p (n t)"))
+            (nc.scalar if c == len(B_CHUNKS) - 1 else nc.sync).dma_start(out=words_out[:, cols], in_=o_words[:, cols].bitcast(I32))
+        scales_out = out_2[0].bitcast(I32)
+        for q in range(4):
+            queue = nc.sync if q % 2 == 0 else nc.scalar
+            queue.dma_start(out=scales_out[4 * q : 4 * q + 4, :], in_=o_scales[32 * q : 32 * q + 4, :].bitcast(I32))

@@ -90,6 +90,11 @@ def tile_picked_twkeyjointbtrack_none_po_kernel(
         gain = keep.tile([P, PACK], F32, name="gain")
         nc.gpsimd.dma_start(out=gain[:], in_=gn.rearrange("(p t) o -> p (t o)", t=PACK))
 
+        warm_in = keep.tile([P, 1], F32, name="warm_in")
+        warm_out = keep.tile([P, 1], F32, name="warm_out")
+        nc.vector.memset(warm_in[:], 0.0)
+        nc.scalar.activation(out=warm_out[:], in_=warm_in[:], func=ACT.Sigmoid)
+
         ds_placed = keep.tile([P, H], U8, name="ds_placed", align_bytes=64)
         nc.vector.memset(ds_placed[:].bitcast(I32), 0)
         ds_got = keep.tile([P, H], U8, name="ds_got", align_bytes=64)

@@ -17,14 +17,9 @@ ALU = mybir.AluOpType
 
 P = 128
 PACK = 4
-A_CHUNKS = [256, 128, 128]
-A_SKEW = 3
-B_CHUNKS = [128, 256, 128]
-
-
-def chunk_slices(widths):
-    starts = [sum(widths[:c]) for c in range(len(widths))]
-    return [slice(a, a + w) for a, w in zip(starts, widths)]
+HALF = S // 2
+HALVES = [slice(0, HALF), slice(HALF, S)]
+PAIRS = [slice(0, 2), slice(2, 4)]
 
 
 def entries(list_tile, cols):
@@ -43,7 +38,7 @@ def deal(engine_copy, dst, src, run):
 
 
 def interleave(engine_copy, dst, src):
-    engine_copy(out=dst[:].rearrange("p (c i) t -> p c t i", i=4), in_=src[:].rearrange("p t (c i) -> p c t i", i=4))
+    engine_copy(out=dst.rearrange("p (c i) t -> p c t i", i=4), in_=src.rearrange("p t (c i) -> p c t i", i=4))
 
 
 def tile_picked_twkeyjointbtrack_none_po_kernel(
@@ -60,6 +55,11 @@ def tile_picked_twkeyjointbtrack_none_po_kernel(
             nc.sync.dma_start(held[:], dram)
             return held
 
+        def load_words(name, dram, columns, tag):
+            held = keep.tile([P, columns], U32, name=name, tag=tag, align_bytes=64)
+            nc.sync.dma_start(out=held[:].bitcast(I32), in_=words_of(dram))
+            return held
+
         k1_l = load_list("k1_l", k1)
         ds_win = keep.tile([P, G], U8, name="ds_win", align_bytes=64)
         ds_src = d_scales[0].bitcast(I32).rearrange("(g e) c -> e g c", e=2)
@@ -71,22 +71,15 @@ def tile_picked_twkeyjointbtrack_none_po_kernel(
             queue = nc.gpsimd if r == 3 else nc.sync
             queue.dma_start(out=xs_win[r:P:4, :].bitcast(I32), in_=xs_src[r].unsqueeze(1).to_broadcast([4, 8, T // 4]))
         two_l = load_list("two_l", two)
-        dw_win = keep.tile([P, G], U32, name="dw_win", align_bytes=64)
-        nc.sync.dma_start(out=dw_win[:].bitcast(I32), in_=words_of(d_words))
+        dw_win = load_words("dw_win", d_words, G, "dw_win")
+
         offs_l = load_list("offs_l", offs)
+        xw_win = load_words("xw_win", x_words, T, "xw_win")
+        w1_raw = load_words("w1_raw", w1_words, H, "w1_then_d0")
         n2_l = load_list("n2_l", n2)
-        ws_raw = keep.tile([P, H], U8, name="ws_raw", tag="slot_b", align_bytes=64)
-
-        def load_weight_scales(rows):
-            for row in rows:
-                src = (w1_scales, w2_scales)[row // 4][0].bitcast(I32).rearrange("(q r) c -> r q c", r=4)
-                nc.sync.dma_start(out=ws_raw[row:P:8, :].bitcast(I32), in_=src[row % 4].unsqueeze(1).to_broadcast([4, 4, H // 4]))
-
-        load_weight_scales(range(2))
-        w1_raw = keep.tile([P, H], U32, name="w1_raw", tag="slot_a", align_bytes=64)
-        nc.sync.dma_start(out=w1_raw[:].bitcast(I32), in_=words_of(w1_words))
-        xw_win = keep.tile([P, T], U32, name="xw_win", align_bytes=64)
-        nc.sync.dma_start(out=xw_win[:].bitcast(I32), in_=words_of(x_words))
+        n1_l = load_list("n1_l", n1)
+        n3_l = load_list("n3_l", n3)
+        n4_l = load_list("n4_l", n4)
         gain = keep.tile([P, PACK], F32, name="gain")
         nc.gpsimd.dma_start(out=gain[:], in_=gn.rearrange("(p t) o -> p (t o)", t=PACK))
 
@@ -97,9 +90,9 @@ def tile_picked_twkeyjointbtrack_none_po_kernel(
 
         ds_placed = keep.tile([P, H], U8, name="ds_placed", align_bytes=64)
         nc.vector.memset(ds_placed[:].bitcast(I32), 0)
-        ds_got = keep.tile([P, H], U8, name="ds_got", align_bytes=64)
+        ds_got = keep.tile([P, H], U8, name="ds_got", tag="got_ws_diff", align_bytes=64)
         nc.vector.tensor_copy(out=ds_got[:], in_=ds_win[:].indirect(k1_l[:]))
-        ds_dealt = keep.tile([P, H], U8, name="ds_dealt", align_bytes=64)
+        ds_dealt = keep.tile([P, H], U8, name="ds_dealt", tag="dealt_w2_dn2", align_bytes=64)
         deal(nc.vector.tensor_copy, ds_dealt, ds_got, 16)
         nc.scalar.dma_start(out=ds_placed[0:112, :].bitcast(I32), in_=ds_dealt[14:126, :].bitcast(I32))
 
@@ -123,14 +116,16 @@ def tile_picked_twkeyjointbtrack_none_po_kernel(
         xw_idx = keep.tile([P, S], U32, name="xw_idx", align_bytes=64)
         nc.vector.tensor_copy(out=xw_idx[:], in_=xw_win[:].indirect(offs_l[:]))
 
-        load_weight_scales(range(2, 8))
-        n1_l = load_list("n1_l", n1)
-        w2_raw = keep.tile([P, N], U32, name="w2_raw", tag="slot_c", align_bytes=64)
-        nc.sync.dma_start(out=w2_raw[:].bitcast(I32), in_=words_of(w2_words))
-        n3_l = load_list("n3_l", n3)
-        n4_l = load_list("n4_l", n4)
+        ws_raw = keep.tile([P, H], U8, name="ws_raw", tag="got_ws_diff", align_bytes=64)
+        for w, scales in enumerate((w1_scales, w2_scales)):
+            ws_src = scales[0].bitcast(I32).rearrange("(q r) c -> r q c", r=4)
+            for r in range(4):
+                nc.sync.dma_start(out=ws_raw[4 * w + r : P : 8, :].bitcast(I32), in_=ws_src[r].unsqueeze(1).to_broadcast([4, 4, H // 4]))
+        w2_raw = load_words("w2_raw", w2_words, N, "dealt_w2_dn2")
         w1_dealt = keep.tile([P, H], U32, name="w1_dealt", align_bytes=64)
         deal(nc.scalar.copy, w1_dealt, w1_raw, 4)
+        w2_dealt = keep.tile([P, N], U32, name="w2_dealt", align_bytes=64)
+        deal(nc.scalar.copy, w2_dealt, w2_raw, 4)
         ws_dealt = keep.tile([P, H], U8, name="ws_dealt", align_bytes=64)
         deal(nc.vector.tensor_copy, ws_dealt, ws_raw, 16)
 
@@ -140,77 +135,87 @@ def tile_picked_twkeyjointbtrack_none_po_kernel(
             nc.tensor.matmul_mx(out=y_ps[t][:], lhsT=w1_dealt[:, m].bitcast(FP8X4), lhsT_scale=ws_dealt[:, m],
                                 rhs=xw_idx[:].bitcast(FP8X4), rhs_scale=xs_idx[:], start=True, stop=True)
 
-        d_win = [keep.tile([P, S], F32, name=f"d_win{t}", tag="slot_a" if t == 0 else f"d_win{t}", align_bytes=64) for t in range(PACK)]
+        d_tags = ["w1_then_d0", "d_win1", "d_win2", "d_win3"]
+        d_win = [keep.tile([P, S], F32, name=f"d_win{t}", tag=d_tags[t], align_bytes=64) for t in range(PACK)]
         h_win = [keep.tile([P, S], F32, name=f"h_win{t}") for t in range(PACK)]
-        h_ps = [psum.tile([P, S], F32, name=f"h_ps{t}", tag=f"bank{t}") for t in range(PACK)]
-        w2_dealt = keep.tile([P, N], U32, name="w2_dealt", align_bytes=64)
-
-        for c, cols in enumerate(chunk_slices(A_CHUNKS)):
-            width = cols.stop - cols.start
-            d_two = keep.tile([P, PACK, width], F32, name=f"d_two{c}", tag="slot_c" if c == 1 else f"d_two{c}", align_bytes=64)
-            diff = keep.tile([P, PACK, width], F32, name=f"diff{c}", tag="slot_b" if c == 0 else f"diff{c}", align_bytes=64)
-            bend = keep.tile([P, PACK, width], F32, name=f"bend{c}")
-            z_rows = keep.tile([P, PACK, width], BF16, name=f"z_rows{c}")
-            for t in range(PACK + A_SKEW):
-                if t < PACK:
-                    if c == 0:
-                        nc.scalar.copy(out=d_win[t][:], in_=d_ps[t][:])
-                    nc.scalar.activation(out=d_two[:, t, :], in_=d_win[t][:].indirect(entries(n2_l, cols)), func=ACT.Copy)
-                    nc.vector.tensor_tensor(out=diff[:, t, :], in0=d_win[t][:].indirect(entries(n1_l, cols)), in1=d_two[:, t, :], op=ALU.subtract)
-                if t >= A_SKEW:
-                    u = t - A_SKEW
-                    nc.scalar.activation(out=bend[:, u, :], in_=diff[:, u, :], func=ACT.Tanh, scale=0.0625)
-                    nc.vector.scalar_tensor_tensor(out=z_rows[:, u, :], in0=y_ps[u][:, cols], scalar=gain[:, u : u + 1], in1=bend[:, u, :], op0=ALU.mult, op1=ALU.mult)
-            if c == 0:
-                deal(nc.scalar.copy, w2_dealt, w2_raw, 4)
-            z_packed = keep.tile([P, width, PACK], BF16, name=f"z_packed{c}", align_bytes=64)
-            interleave(nc.scalar.copy if c == 1 else nc.vector.tensor_copy, z_packed, z_rows)
-            z_words = keep.tile([P, width], U32, name=f"z_words{c}", align_bytes=64)
-            z_scales = keep.tile([P, width], U8, name=f"z_scales{c}", align_bytes=64)
+        z_quantised = []
+        for c, cols in enumerate(HALVES):
+            d_n2 = keep.tile([P, PACK, HALF], F32, name=f"d_n2_{c}", tag="dealt_w2_dn2" if c == 1 else "d_n2_0", align_bytes=64)
+            diff = keep.tile([P, PACK, HALF], F32, name=f"diff{c}", tag="got_ws_diff" if c == 0 else "diff1", align_bytes=64)
+            bend = keep.tile([P, PACK, HALF], F32, name=f"bend{c}")
+            z_rows = keep.tile([P, PACK, HALF], BF16, name=f"z_rows{c}")
+            for t in range(PACK):
+                if c == 0:
+                    leave = nc.vector.tensor_copy if t == 1 else nc.scalar.copy
+                    leave(out=d_win[t][:], in_=d_ps[t][:])
+                nc.scalar.activation(out=d_n2[:, t, :], in_=d_win[t][:].indirect(entries(n2_l, cols)), func=ACT.Copy)
+                nc.vector.tensor_tensor(out=diff[:, t, :], in0=d_win[t][:].indirect(entries(n1_l, cols)), in1=d_n2[:, t, :], op=ALU.subtract)
+            step = 2 if c == 0 else 1
+            for first in range(0, PACK, step):
+                nc.scalar.activation(out=bend[:, first : first + step, :], in_=diff[:, first : first + step, :], func=ACT.Tanh, scale=0.0625)
+                for t in range(first, first + step):
+                    nc.vector.scalar_tensor_tensor(out=z_rows[:, t, :], in0=y_ps[t][:, cols], scalar=gain[:, t : t + 1], in1=bend[:, t, :], op0=ALU.mult, op1=ALU.mult)
+            z_packed = keep.tile([P, HALF, PACK], BF16, name=f"z_packed{c}", align_bytes=64)
+            interleave(nc.vector.tensor_copy, z_packed[:], z_rows[:])
+            z_words = keep.tile([P, HALF], U32, name=f"z_words{c}", align_bytes=64)
+            z_scales = keep.tile([P, HALF], U8, name=f"z_scales{c}", align_bytes=64)
             nc.vector.quantize_mx(out=z_words[:].bitcast(FP8X4), scales=z_scales[:], in_=z_packed[:].rearrange("p n t -> p (n t)"))
+            z_quantised.append((z_words, z_scales))
+
+        h_ps = []
+        for c, cols in enumerate(HALVES):
+            z_words, z_scales = z_quantised[c]
+            banks = [psum.tile([P, 2, HALF], F32, name=f"h_ps{c}{j}", tag=f"bank{2 * c + j}") for j in range(2)]
+            h_ps.append(banks)
             for t in range(PACK):
                 m = slice(t * P, (t + 1) * P)
-                nc.tensor.matmul_mx(out=h_ps[t][:, cols], lhsT=w2_dealt[:, m].bitcast(FP8X4), lhsT_scale=ws_dealt[4:P, m],
+                nc.tensor.matmul_mx(out=banks[t // 2][:, t % 2, :], lhsT=w2_dealt[:, m].bitcast(FP8X4), lhsT_scale=ws_dealt[4:P, m],
                                     rhs=z_words[:].bitcast(FP8X4), rhs_scale=z_scales[:], start=True, stop=True)
             for t in range(PACK):
-                leave = nc.vector.tensor_copy if (c == len(A_CHUNKS) - 1 and t > 0) else nc.scalar.copy
-                leave(out=h_win[t][:, cols], in_=h_ps[t][:, cols])
+                leave = nc.vector.tensor_copy if (c == 1 and t > 0) else nc.scalar.copy
+                leave(out=h_win[t][:, cols], in_=banks[t // 2][:, t % 2, :])
 
         out_rows = out_0.rearrange("(p t) n -> p t n", t=PACK)
         o_words = keep.tile([P, S], U32, name="o_words", align_bytes=64)
         o_scales = keep.tile([P, S], U8, name="o_scales", align_bytes=64)
-        words_out = words_of(out_1)
-        for c, cols in enumerate(chunk_slices(B_CHUNKS)):
-            width = cols.stop - cols.start
-            gate = keep.tile([P, PACK, width], F32, name=f"gate{c}")
-            got = keep.tile([P, PACK, width], F32, name=f"got{c}") if c == 1 else None
-            far = keep.tile([P, PACK, width], F32, name=f"far{c}")
-            near = keep.tile([P, PACK, width], F32, name=f"near{c}")
-            mixed = keep.tile([P, PACK, width], F32, name=f"mixed{c}")
-            for t in range(PACK + 1):
-                if t < PACK:
-                    nc.scalar.activation(out=gate[:, t, :], in_=h_win[t][:].indirect(entries(n3_l, cols)), func=ACT.Sigmoid)
-                    if c == 1:
-                        nc.scalar.activation(out=got[:, t, :], in_=h_win[t][:].indirect(entries(n4_l, cols)), func=ACT.Copy)
-                        nc.vector.tensor_tensor(out=near[:, t, :], in0=got[:, t, :], in1=h_win[t][:, cols], op=ALU.subtract)
-                        nc.vector.tensor_tensor(out=far[:, t, :], in0=near[:, t, :], in1=gate[:, t, :], op=ALU.mult)
-                    else:
-                        nc.vector.tensor_tensor(out=far[:, t, :], in0=h_win[t][:].indirect(entries(n4_l, cols)), in1=gate[:, t, :], op=ALU.mult)
-                        nc.vector.scalar_tensor_tensor(out=near[:, t, :], in0=gate[:, t, :], scalar=1.0, in1=h_win[t][:, cols], op0=ALU.subtract, op1=ALU.mult)
-                if t > 0:
-                    u = t - 1
-                    if c == 1:
-                        nc.vector.tensor_tensor(out=mixed[:, u, :], in0=far[:, u, :], in1=h_win[u][:, cols], op=ALU.add)
-                        if u % 2 == 1:
-                            nc.sync.dma_start(out=out_rows[:, u - 1 : u + 1, cols], in_=mixed[:, u - 1 : u + 1, :])
-                    else:
-                        nc.vector.tensor_tensor(out=mixed[:, u, :], in0=far[:, u, :], in1=near[:, u, :], op=ALU.subtract)
-            if c != 1:
-                nc.sync.dma_start(out=out_rows[:, :, cols], in_=mixed[:])
-            o_packed = keep.tile([P, width, PACK], BF16, name=f"o_packed{c}", align_bytes=64)
-            interleave(nc.scalar.copy if c == 1 else nc.vector.tensor_copy, o_packed, mixed)
-            nc.vector.quantize_mx(out=o_words[:, cols].bitcast(FP8X4), scales=o_scales[:, cols], in_=o_packed[:].rearrange("p n t -> p (n t)"))
-            (nc.scalar if c == len(B_CHUNKS) - 1 else nc.sync).dma_start(out=words_out[:, cols], in_=o_words[:, cols].bitcast(I32))
+        gate = [keep.tile([P, PACK, HALF], F32, name=f"gate{c}") for c in range(2)]
+        far = [keep.tile([P, PACK, HALF], F32, name=f"far{c}") for c in range(2)]
+        near = [keep.tile([P, PACK, HALF], F32, name=f"near{c}") for c in range(2)]
+        mixed = [keep.tile([P, PACK, HALF], F32, name=f"mixed{c}") for c in range(2)]
+        pull = keep.tile([P, PACK, HALF], F32, name="pull")
+
+        def fetch_gate(c, t):
+            nc.scalar.activation(out=gate[c][:, t, :], in_=h_win[t][:].indirect(entries(n3_l, HALVES[c])), func=ACT.Sigmoid)
+
+        def fetch_far(t):
+            nc.scalar.activation(out=far[1][:, t, :], in_=h_win[t][:].indirect(entries(n4_l, HALVES[1])), func=ACT.Copy)
+
+        for t in range(PACK):
+            fetch_gate(0, t)
+            nc.vector.tensor_tensor(out=far[0][:, t, :], in0=h_win[t][:].indirect(entries(n4_l, HALVES[0])), in1=gate[0][:, t, :], op=ALU.mult)
+        for j, pair in enumerate(PAIRS):
+            nc.vector.scalar_tensor_tensor(out=near[0][:, pair, :], in0=gate[0][:, pair, :], scalar=1.0, in1=h_ps[0][j][:], op0=ALU.subtract, op1=ALU.mult)
+        for pair in PAIRS:
+            nc.vector.tensor_tensor(out=mixed[0][:, pair, :], in0=far[0][:, pair, :], in1=near[0][:, pair, :], op=ALU.subtract)
+            nc.sync.dma_start(out=out_rows[:, pair, HALVES[0]], in_=mixed[0][:, pair, :])
+
+        for j, pair in enumerate(PAIRS):
+            for t in range(pair.start, pair.stop):
+                fetch_far(t)
+            for t in range(pair.start, pair.stop):
+                fetch_gate(1, t)
+            nc.vector.tensor_tensor(out=near[1][:, pair, :], in0=far[1][:, pair, :], in1=h_ps[1][j][:], op=ALU.subtract)
+        for rows in (slice(0, 2), slice(2, 3), slice(3, 4)):
+            h_rows = h_ps[1][rows.start // 2][:, rows.start % 2 : rows.start % 2 + rows.stop - rows.start, :]
+            nc.vector.tensor_tensor(out=pull[:, rows, :], in0=near[1][:, rows, :], in1=gate[1][:, rows, :], op=ALU.mult)
+            nc.vector.tensor_tensor(out=mixed[1][:, rows, :], in0=pull[:, rows, :], in1=h_rows, op=ALU.add)
+        for pair in PAIRS:
+            nc.sync.dma_start(out=out_rows[:, pair, HALVES[1]], in_=mixed[1][:, pair, :])
+        o_packed = keep.tile([P, S, PACK], BF16, name="o_packed", align_bytes=64)
+        interleave(nc.scalar.copy, o_packed[:, HALVES[0], :], mixed[0][:])
+        interleave(nc.vector.tensor_copy, o_packed[:, HALVES[1], :], mixed[1][:])
+        nc.vector.quantize_mx(out=o_words[:].bitcast(FP8X4), scales=o_scales[:], in_=o_packed[:].rearrange("p n t -> p (n t)"))
+        nc.scalar.dma_start(out=words_of(out_1), in_=o_words[:].bitcast(I32))
         scales_out = out_2[0].bitcast(I32)
         for q in range(4):
             queue = nc.sync if q % 2 == 0 else nc.scalar

@@ -62,23 +62,19 @@ def tile_picked_twkeyjointbtrack_none_po_kernel(
 
         k1_l = load_list("k1_l", k1)
         ds_win = keep.tile([P, G], U8, name="ds_win", align_bytes=64)
-        ds_src = d_scales[0].bitcast(I32).rearrange("(g e) c -> e g c", e=2)
-        for e in range(2):
-            nc.sync.dma_start(out=ds_win[e:P:2, :].bitcast(I32), in_=ds_src[e].unsqueeze(1).to_broadcast([8, 8, G // 4]))
-        xs_win = keep.tile([P, T], U8, name="xs_win", align_bytes=64)
-        xs_src = x_scales[0].bitcast(I32).rearrange("(q r) c -> r q c", r=4)
-        for r in range(4):
-            queue = nc.gpsimd if r == 3 else nc.sync
-            queue.dma_start(out=xs_win[r:P:4, :].bitcast(I32), in_=xs_src[r].unsqueeze(1).to_broadcast([4, 8, T // 4]))
+        nc.scalar.dma_start(out=ds_win[:].bitcast(I32), in_=d_scales[0].bitcast(I32).unsqueeze(1).to_broadcast([16, 8, G // 4]))
         two_l = load_list("two_l", two)
-        dw_win = load_words("dw_win", d_words, G, "dw_win")
-
         offs_l = load_list("offs_l", offs)
-        xw_win = load_words("xw_win", x_words, T, "xw_win")
-        w1_raw = load_words("w1_raw", w1_words, H, "w1_then_d0")
         n2_l = load_list("n2_l", n2)
         n1_l = load_list("n1_l", n1)
         n3_l = load_list("n3_l", n3)
+        dw_win = load_words("dw_win", d_words, G, "dw_win")
+        xs_win = keep.tile([P, T], U8, name="xs_win", align_bytes=64)
+        nc.vector.memset(xs_win[:].bitcast(I32), 0)
+        for r in range(4):
+            nc.sync.dma_start(out=xs_win[r:P:32, :].bitcast(I32), in_=x_scales[0].bitcast(I32)[r:16:4, :])
+        xw_win = load_words("xw_win", x_words, T, "xw_w2_dn2")
+        w1_raw = load_words("w1_raw", w1_words, H, "w1_then_d0")
         n4_l = load_list("n4_l", n4)
         gain = keep.tile([P, PACK], F32, name="gain")
         nc.gpsimd.dma_start(out=gain[:], in_=gn.rearrange("(p t) o -> p (t o)", t=PACK))
@@ -88,27 +84,26 @@ def tile_picked_twkeyjointbtrack_none_po_kernel(
         nc.vector.memset(warm_in[:], 0.0)
         nc.scalar.activation(out=warm_out[:], in_=warm_in[:], func=ACT.Sigmoid)
 
-        ds_placed = keep.tile([P, H], U8, name="ds_placed", align_bytes=64)
-        nc.vector.memset(ds_placed[:].bitcast(I32), 0)
-        ds_got = keep.tile([P, H], U8, name="ds_got", tag="got_ws_diff", align_bytes=64)
+        ds_got = keep.tile([P, H], U8, name="ds_got", align_bytes=64)
         nc.vector.tensor_copy(out=ds_got[:], in_=ds_win[:].indirect(k1_l[:]))
-        ds_dealt = keep.tile([P, H], U8, name="ds_dealt", tag="dealt_w2_dn2", align_bytes=64)
+        ds_dealt = keep.tile([P, H], U8, name="ds_dealt", align_bytes=64)
         deal(nc.vector.tensor_copy, ds_dealt, ds_got, 16)
-        nc.scalar.dma_start(out=ds_placed[0:112, :].bitcast(I32), in_=ds_dealt[14:126, :].bitcast(I32))
+        for r in range(1, 4):
+            nc.scalar.dma_start(out=ds_dealt[r:P:32, :].bitcast(I32), in_=ds_dealt[8 * r : P : 32, :].bitcast(I32))
 
-        xs_two = keep.tile([P, S], U8, name="xs_two", align_bytes=64)
-        nc.vector.tensor_copy(out=xs_two[:], in_=xs_win[:].indirect(two_l[:]))
-        dw_got = keep.tile([P, H], U32, name="dw_got", align_bytes=64)
+        dw_got = keep.tile([P, H], U32, name="dw_got", tag="got_ws_diff", align_bytes=64)
         nc.vector.tensor_copy(out=dw_got[:], in_=dw_win[:].indirect(k1_l[:]))
         dw_dealt = keep.tile([P, H], U32, name="dw_dealt", align_bytes=64)
         deal(nc.vector.tensor_copy, dw_dealt, dw_got, 4)
+        xs_two = keep.tile([P, S], U8, name="xs_two", align_bytes=64)
+        nc.vector.tensor_copy(out=xs_two[:], in_=xs_win[:].indirect(two_l[:]))
         xw_two = keep.tile([P, S], U32, name="xw_two", align_bytes=64)
         nc.vector.tensor_copy(out=xw_two[:], in_=xw_win[:].indirect(two_l[:]))
 
         d_ps = [psum.tile([P, S], F32, name=f"d_ps{t}", tag=f"bank{t}") for t in range(PACK)]
         for t in range(PACK):
             m = slice(t * P, (t + 1) * P)
-            nc.tensor.matmul_mx(out=d_ps[t][:], lhsT=dw_dealt[:, m].bitcast(FP8X4), lhsT_scale=ds_placed[:, m],
+            nc.tensor.matmul_mx(out=d_ps[t][:], lhsT=dw_dealt[:, m].bitcast(FP8X4), lhsT_scale=ds_dealt[:, m],
                                 rhs=xw_two[:].bitcast(FP8X4), rhs_scale=xs_two[:], start=True, stop=True)
 
         xs_idx = keep.tile([P, S], U8, name="xs_idx", align_bytes=64)
@@ -117,11 +112,11 @@ def tile_picked_twkeyjointbtrack_none_po_kernel(
         nc.vector.tensor_copy(out=xw_idx[:], in_=xw_win[:].indirect(offs_l[:]))
 
         ws_raw = keep.tile([P, H], U8, name="ws_raw", tag="got_ws_diff", align_bytes=64)
+        nc.vector.memset(ws_raw[:].bitcast(I32), 0)
         for w, scales in enumerate((w1_scales, w2_scales)):
-            ws_src = scales[0].bitcast(I32).rearrange("(q r) c -> r q c", r=4)
             for r in range(4):
-                nc.sync.dma_start(out=ws_raw[4 * w + r : P : 8, :].bitcast(I32), in_=ws_src[r].unsqueeze(1).to_broadcast([4, 4, H // 4]))
-        w2_raw = load_words("w2_raw", w2_words, N, "dealt_w2_dn2")
+                nc.sync.dma_start(out=ws_raw[4 * w + r : P : 32, :].bitcast(I32), in_=scales[0].bitcast(I32)[r:16:4, :])
+        w2_raw = load_words("w2_raw", w2_words, N, "xw_w2_dn2")
         w1_dealt = keep.tile([P, H], U32, name="w1_dealt", align_bytes=64)
         deal(nc.scalar.copy, w1_dealt, w1_raw, 4)
         w2_dealt = keep.tile([P, N], U32, name="w2_dealt", align_bytes=64)
@@ -140,7 +135,7 @@ def tile_picked_twkeyjointbtrack_none_po_kernel(
         h_win = [keep.tile([P, S], F32, name=f"h_win{t}") for t in range(PACK)]
         z_quantised = []
         for c, cols in enumerate(HALVES):
-            d_n2 = keep.tile([P, PACK, HALF], F32, name=f"d_n2_{c}", tag="dealt_w2_dn2" if c == 1 else "d_n2_0", align_bytes=64)
+            d_n2 = keep.tile([P, PACK, HALF], F32, name=f"d_n2_{c}", tag="xw_w2_dn2" if c == 1 else "d_n2_0", align_bytes=64)
             diff = keep.tile([P, PACK, HALF], F32, name=f"diff{c}", tag="got_ws_diff" if c == 0 else "diff1", align_bytes=64)
             bend = keep.tile([P, PACK, HALF], F32, name=f"bend{c}")
             z_rows = keep.tile([P, PACK, HALF], BF16, name=f"z_rows{c}")

from contextlib import ExitStack

import concourse.mybir as mybir

K, T, S, N, H, G = 512, 2048, 512, 512, 512, 2048
FLOPS = 2 * K * H * S * 2 + 2 * H * N * S

F32 = mybir.dt.float32
BF16 = mybir.dt.bfloat16
I32 = mybir.dt.int32
U32 = mybir.dt.uint32
U16 = mybir.dt.uint16
U8 = mybir.dt.uint8
FP8X4 = mybir.dt.float8_e4m3fn_x4
ACT = mybir.ActivationFunctionType
ALU = mybir.AluOpType

P = 128
PACK = 4
HALF = S // 2
HALVES = [slice(0, HALF), slice(HALF, S)]
PAIRS = [slice(0, 2), slice(2, 4)]


def entries(list_tile, cols):
    return list_tile[:, cols.start // 16 : cols.stop // 16]


def words_of(dram):
    return dram[0].rearrange("p n t -> p (n t)").bitcast(I32)


def deal(engine_copy, dst, src, run):
    engine_copy(
        out=dst[:].rearrange("p (t c i) -> p c t i", t=PACK, i=run),
        in_=src[:].rearrange("p (c i t) -> p c t i", t=PACK, i=run),
    )


def interleave(engine_copy, dst, src):
    engine_copy(out=dst.rearrange("p (c i) t -> p c t i", i=4), in_=src.rearrange("p t (c i) -> p c t i", i=4))


def tile_picked_twkeyjointbtrack_none_po_kernel(
    tc, x_words, x_scales, w1_words, w1_scales, d_words, d_scales, gn, w2_words, w2_scales, offs, k1, two, n1, n2, n3, n4, out_0, out_1, out_2
):
    nc = tc.nc
    with ExitStack() as ctx:
        lists = ctx.enter_context(tc.tile_pool(name="lists", bufs=1))
        keep = ctx.enter_context(tc.tile_pool(name="keep", bufs=1))
        psum = ctx.enter_context(tc.psum_pool(name="psum", bufs=1))

        def load_list(name, dram):
            held = lists.tile([P, S // 16], U16, name=name)
            nc.sync.dma_start(held[:], dram)
            return held

        def load_words(name, dram, columns, tag):
            held = keep.tile([P, columns], U32, name=name, tag=tag, align_bytes=64)
            nc.sync.dma_start(out=held[:].bitcast(I32), in_=words_of(dram))
            return held

        k1_l = load_list("k1_l", k1)
        ds_win = keep.tile([P, G], U8, name="ds_win", align_bytes=64)
        nc.scalar.dma_start(out=ds_win[:].bitcast(I32), in_=d_scales[0].bitcast(I32).unsqueeze(1).to_broadcast([16, 8, G // 4]))
        two_l = load_list("two_l", two)
        offs_l = load_list("offs_l", offs)
        n2_l = load_list("n2_l", n2)
        n1_l = load_list("n1_l", n1)
        n3_l = load_list("n3_l", n3)
        dw_win = load_words("dw_win", d_words, G, "dw_win")
        xs_win = keep.tile([P, T], U8, name="xs_win", align_bytes=64)
        nc.vector.memset(xs_win[:].bitcast(I32), 0)
        for r in range(4):
            nc.sync.dma_start(out=xs_win[r:P:32, :].bitcast(I32), in_=x_scales[0].bitcast(I32)[r:16:4, :])
        xw_win = load_words("xw_win", x_words, T, "xw_w2_dn2")
        w1_raw = load_words("w1_raw", w1_words, H, "w1_then_d0")
        n4_l = load_list("n4_l", n4)
        gain = keep.tile([P, PACK], F32, name="gain")
        nc.gpsimd.dma_start(out=gain[:], in_=gn.rearrange("(p t) o -> p (t o)", t=PACK))

        warm_in = keep.tile([P, 1], F32, name="warm_in")
        warm_out = keep.tile([P, 1], F32, name="warm_out")
        nc.vector.memset(warm_in[:], 0.0)
        nc.scalar.activation(out=warm_out[:], in_=warm_in[:], func=ACT.Sigmoid)

        ds_got = keep.tile([P, H], U8, name="ds_got", align_bytes=64)
        nc.vector.tensor_copy(out=ds_got[:], in_=ds_win[:].indirect(k1_l[:]))
        ds_dealt = keep.tile([P, H], U8, name="ds_dealt", align_bytes=64)
        deal(nc.vector.tensor_copy, ds_dealt, ds_got, 16)
        for r in range(1, 4):
            nc.scalar.dma_start(out=ds_dealt[r:P:32, :].bitcast(I32), in_=ds_dealt[8 * r : P : 32, :].bitcast(I32))

        dw_got = keep.tile([P, H], U32, name="dw_got", tag="got_ws_diff", align_bytes=64)
        nc.vector.tensor_copy(out=dw_got[:], in_=dw_win[:].indirect(k1_l[:]))
        dw_dealt = keep.tile([P, H], U32, name="dw_dealt", align_bytes=64)
        deal(nc.vector.tensor_copy, dw_dealt, dw_got, 4)
        xs_two = keep.tile([P, S], U8, name="xs_two", align_bytes=64)
        nc.vector.tensor_copy(out=xs_two[:], in_=xs_win[:].indirect(two_l[:]))
        xw_two = keep.tile([P, S], U32, name="xw_two", align_bytes=64)
        nc.vector.tensor_copy(out=xw_two[:], in_=xw_win[:].indirect(two_l[:]))

        d_ps = [psum.tile([P, S], F32, name=f"d_ps{t}", tag=f"bank{t}") for t in range(PACK)]
        for t in range(PACK):
            m = slice(t * P, (t + 1) * P)
            nc.tensor.matmul_mx(out=d_ps[t][:], lhsT=dw_dealt[:, m].bitcast(FP8X4), lhsT_scale=ds_dealt[:, m],
                                rhs=xw_two[:].bitcast(FP8X4), rhs_scale=xs_two[:], start=True, stop=True)

        xs_idx = keep.tile([P, S], U8, name="xs_idx", align_bytes=64)
        nc.vector.tensor_copy(out=xs_idx[:], in_=xs_win[:].indirect(offs_l[:]))
        xw_idx = keep.tile([P, S], U32, name="xw_idx", align_bytes=64)
        nc.vector.tensor_copy(out=xw_idx[:], in_=xw_win[:].indirect(offs_l[:]))

        ws_raw = keep.tile([P, H], U8, name="ws_raw", tag="got_ws_diff", align_bytes=64)
        nc.vector.memset(ws_raw[:].bitcast(I32), 0)
        for w, scales in enumerate((w1_scales, w2_scales)):
            for r in range(4):
                nc.sync.dma_start(out=ws_raw[4 * w + r : P : 32, :].bitcast(I32), in_=scales[0].bitcast(I32)[r:16:4, :])
        w2_raw = load_words("w2_raw", w2_words, N, "xw_w2_dn2")
        w1_dealt = keep.tile([P, H], U32, name="w1_dealt", align_bytes=64)
        deal(nc.scalar.copy, w1_dealt, w1_raw, 4)
        w2_dealt = keep.tile([P, N], U32, name="w2_dealt", align_bytes=64)
        deal(nc.scalar.copy, w2_dealt, w2_raw, 4)
        ws_dealt = keep.tile([P, H], U8, name="ws_dealt", align_bytes=64)
        deal(nc.vector.tensor_copy, ws_dealt, ws_raw, 16)

        y_ps = [psum.tile([P, S], F32, name=f"y_ps{t}", tag=f"bank{PACK + t}") for t in range(PACK)]
        for t in range(PACK):
            m = slice(t * P, (t + 1) * P)
            nc.tensor.matmul_mx(out=y_ps[t][:], lhsT=w1_dealt[:, m].bitcast(FP8X4), lhsT_scale=ws_dealt[:, m],
                                rhs=xw_idx[:].bitcast(FP8X4), rhs_scale=xs_idx[:], start=True, stop=True)

        d_tags = ["w1_then_d0", "d_win1", "d_win2", "d_win3"]
        d_win = [keep.tile([P, S], F32, name=f"d_win{t}", tag=d_tags[t], align_bytes=64) for t in range(PACK)]
        h_win = [keep.tile([P, S], F32, name=f"h_win{t}") for t in range(PACK)]
        z_quantised = []
        for c, cols in enumerate(HALVES):
            d_n2 = keep.tile([P, PACK, HALF], F32, name=f"d_n2_{c}", tag="xw_w2_dn2" if c == 1 else "d_n2_0", align_bytes=64)
            diff = keep.tile([P, PACK, HALF], F32, name=f"diff{c}", tag="got_ws_diff" if c == 0 else "diff1", align_bytes=64)
            bend = keep.tile([P, PACK, HALF], F32, name=f"bend{c}")
            z_rows = keep.tile([P, PACK, HALF], BF16, name=f"z_rows{c}")
            for t in range(PACK):
                if c == 0:
                    leave = nc.vector.tensor_copy if t == 1 else nc.scalar.copy
                    leave(out=d_win[t][:], in_=d_ps[t][:])
                nc.scalar.activation(out=d_n2[:, t, :], in_=d_win[t][:].indirect(entries(n2_l, cols)), func=ACT.Copy)
                nc.vector.tensor_tensor(out=diff[:, t, :], in0=d_win[t][:].indirect(entries(n1_l, cols)), in1=d_n2[:, t, :], op=ALU.subtract)
            step = 2 if c == 0 else 1
            for first in range(0, PACK, step):
                nc.scalar.activation(out=bend[:, first : first + step, :], in_=diff[:, first : first + step, :], func=ACT.Tanh, scale=0.0625)
                for t in range(first, first + step):
                    nc.vector.scalar_tensor_tensor(out=z_rows[:, t, :], in0=y_ps[t][:, cols], scalar=gain[:, t : t + 1], in1=bend[:, t, :], op0=ALU.mult, op1=ALU.mult)
            z_packed = keep.tile([P, HALF, PACK], BF16, name=f"z_packed{c}", align_bytes=64)
            interleave(nc.vector.tensor_copy, z_packed[:], z_rows[:])
            z_words = keep.tile([P, HALF], U32, name=f"z_words{c}", align_bytes=64)
            z_scales = keep.tile([P, HALF], U8, name=f"z_scales{c}", align_bytes=64)
            nc.vector.quantize_mx(out=z_words[:].bitcast(FP8X4), scales=z_scales[:], in_=z_packed[:].rearrange("p n t -> p (n t)"))
            z_quantised.append((z_words, z_scales))

        h_ps = []
        for c, cols in enumerate(HALVES):
            z_words, z_scales = z_quantised[c]
            banks = [psum.tile([P, 2, HALF], F32, name=f"h_ps{c}{j}", tag=f"bank{2 * c + j}") for j in range(2)]
            h_ps.append(banks)
            for t in range(PACK):
                m = slice(t * P, (t + 1) * P)
                nc.tensor.matmul_mx(out=banks[t // 2][:, t % 2, :], lhsT=w2_dealt[:, m].bitcast(FP8X4), lhsT_scale=ws_dealt[4:P, m],
                                    rhs=z_words[:].bitcast(FP8X4), rhs_scale=z_scales[:], start=True, stop=True)
            for t in range(PACK):
                leave = nc.vector.tensor_copy if (c == 1 and t > 0) else nc.scalar.copy
                leave(out=h_win[t][:, cols], in_=banks[t // 2][:, t % 2, :])

        out_rows = out_0.rearrange("(p t) n -> p t n", t=PACK)
        o_words = keep.tile([P, S], U32, name="o_words", align_bytes=64)
        o_scales = keep.tile([P, S], U8, name="o_scales", align_bytes=64)
        gate = [keep.tile([P, PACK, HALF], F32, name=f"gate{c}") for c in range(2)]
        far = [keep.tile([P, PACK, HALF], F32, name=f"far{c}") for c in range(2)]
        near = [keep.tile([P, PACK, HALF], F32, name=f"near{c}") for c in range(2)]
        mixed = [keep.tile([P, PACK, HALF], F32, name=f"mixed{c}") for c in range(2)]
        pull = keep.tile([P, PACK, HALF], F32, name="pull")

        def fetch_gate(c, t):
            nc.scalar.activation(out=gate[c][:, t, :], in_=h_win[t][:].indirect(entries(n3_l, HALVES[c])), func=ACT.Sigmoid)

        def fetch_far(t):
            nc.scalar.activation(out=far[1][:, t, :], in_=h_win[t][:].indirect(entries(n4_l, HALVES[1])), func=ACT.Copy)

        for t in range(PACK):
            fetch_gate(0, t)
            nc.vector.tensor_tensor(out=far[0][:, t, :], in0=h_win[t][:].indirect(entries(n4_l, HALVES[0])), in1=gate[0][:, t, :], op=ALU.mult)
        for j, pair in enumerate(PAIRS):
            nc.vector.scalar_tensor_tensor(out=near[0][:, pair, :], in0=gate[0][:, pair, :], scalar=1.0, in1=h_ps[0][j][:], op0=ALU.subtract, op1=ALU.mult)
        for pair in PAIRS:
            nc.vector.tensor_tensor(out=mixed[0][:, pair, :], in0=far[0][:, pair, :], in1=near[0][:, pair, :], op=ALU.subtract)
            nc.sync.dma_start(out=out_rows[:, pair, HALVES[0]], in_=mixed[0][:, pair, :])

        for j, pair in enumerate(PAIRS):
            for t in range(pair.start, pair.stop):
                fetch_far(t)
            for t in range(pair.start, pair.stop):
                fetch_gate(1, t)
            nc.vector.tensor_tensor(out=near[1][:, pair, :], in0=far[1][:, pair, :], in1=h_ps[1][j][:], op=ALU.subtract)
        for rows in (slice(0, 2), slice(2, 3), slice(3, 4)):
            h_rows = h_ps[1][rows.start // 2][:, rows.start % 2 : rows.start % 2 + rows.stop - rows.start, :]
            nc.vector.tensor_tensor(out=pull[:, rows, :], in0=near[1][:, rows, :], in1=gate[1][:, rows, :], op=ALU.mult)
            nc.vector.tensor_tensor(out=mixed[1][:, rows, :], in0=pull[:, rows, :], in1=h_rows, op=ALU.add)
        for pair in PAIRS:
            nc.sync.dma_start(out=out_rows[:, pair, HALVES[1]], in_=mixed[1][:, pair, :])
        o_packed = keep.tile([P, S, PACK], BF16, name="o_packed", align_bytes=64)
        interleave(nc.scalar.copy, o_packed[:, HALVES[0], :], mixed[0][:])
        interleave(nc.vector.tensor_copy, o_packed[:, HALVES[1], :], mixed[1][:])
        nc.vector.quantize_mx(out=o_words[:].bitcast(FP8X4), scales=o_scales[:], in_=o_packed[:].rearrange("p n t -> p (n t)"))
        nc.scalar.dma_start(out=words_of(out_1), in_=o_words[:].bitcast(I32))
        scales_out = out_2[0].bitcast(I32)
        for q in range(4):
            queue = nc.sync if q % 2 == 0 else nc.scalar
            queue.dma_start(out=scales_out[4 * q : 4 * q + 4, :], in_=o_scales[32 * q : 32 * q + 4, :].bitcast(I32))
